import numpy as np
import ml_dtypes


def mxq(x, axis, fmt="e4m3"):
    dtype, down = {"e4m3": (ml_dtypes.float8_e4m3fn, 7), "e5m2": (ml_dtypes.float8_e5m2, 14)}[fmt]
    v = np.moveaxis(np.asarray(x, np.float32).astype(ml_dtypes.bfloat16).astype(np.float64), axis, -1)
    blocks = v.reshape(v.shape[:-1] + (-1, 32))
    amax = np.abs(blocks).max(-1, keepdims=True)
    byte = np.maximum(np.where(amax > 0, np.frexp(amax)[1] - 1 + 127, 0) - down, 1)
    scale = np.exp2(byte - 127.0)
    codes = (blocks / scale).astype(np.float32).astype(dtype).astype(np.float64)
    return np.moveaxis((codes * scale).reshape(v.shape), -1, axis)


WIDE = False


def mx_kscale(k):
    if not WIDE:
        return np.ones(k)
    levels = np.array([30, -30])
    if k % 512:
        return np.exp2(np.random.permutation(np.resize(levels, k // 32))).repeat(32)
    a = np.empty((k // 512, 16))
    for p in range(k // 512):
        a[p, :8] = np.random.permutation(np.resize(levels, 8))
        for g in range(8):
            far = levels[np.abs(levels - a[p, g]) >= 10]
            a[p, g + 8] = far[np.random.randint(len(far))]
    return np.exp2(a.ravel()).repeat(32)


def f64(x):
    return np.asarray(x).astype(np.float64)


def striped(idx):
    return np.tile(np.asarray(idx).reshape(-1, 16).T, (8, 1)).astype(np.uint16)


def unstriped(offs):
    return offs[:16].T.reshape(-1).astype(np.int64)


E2M1 = np.array([0.0, 0.5, 1.0, 1.5, 2.0, 3.0, 4.0, 6.0, -0.0, -0.5, -1.0, -1.5, -2.0, -3.0, -4.0, -6.0])


def pack_weight(w, fmt):
    k, n = w.shape
    w = f64(np.asarray(w, np.float32).astype(ml_dtypes.bfloat16)).reshape(k // 32, 32, n)
    amax = np.abs(w).max(1)
    if fmt in ("e4m3", "e5m2"):
        byte = np.frexp(amax)[1] - 1 + 127 - (7 if fmt == "e4m3" else 14)
    else:
        mant, ex = np.frexp(amax / 6.0)
        byte = np.where(mant > 0.5, ex, ex - 1) + 127
    byte = np.clip(np.where(amax > 0, byte, 1), 1, 254)
    scaled = (w * np.exp2(127.0 - byte)[:, None, :]).reshape(k, n).astype(np.float32)
    by_word = np.ascontiguousarray(scaled.reshape(k // 512, 128, 4, n).transpose(0, 1, 3, 2))
    if fmt in ("e4m3", "e5m2"):
        words = by_word.astype(ml_dtypes.float8_e4m3fn if fmt == "e4m3" else ml_dtypes.float8_e5m2).view(np.uint8)
    else:
        c = by_word.astype(ml_dtypes.float4_e2m1fn).view(np.uint8) & 0xF
        words = (c[..., 0::2] | (c[..., 1::2] << 4)).reshape(k // 512, 128, 2 * n)
    return np.ascontiguousarray(words), np.ascontiguousarray(byte.astype(np.uint8).reshape(k // 512, 16, n))


def unpack_weight(words, scales, fmt):
    g, _, n = scales.shape
    words = np.ascontiguousarray(words).reshape(g, 128, n, -1)
    if fmt in ("e4m3", "e5m2"):
        vals = words.view(ml_dtypes.float8_e4m3fn if fmt == "e4m3" else ml_dtypes.float8_e5m2).astype(np.float64)
    else:
        nib = np.empty((g, 128, n, 4), np.uint8)
        nib[..., 0::2] = words & 0xF
        nib[..., 1::2] = words >> 4
        vals = E2M1[nib]
    vals = vals * np.repeat(np.exp2(scales.astype(np.float64) - 127.0), 8, axis=1)[..., None]
    return vals.transpose(0, 1, 3, 2).reshape(g * 512, n)


def bf(x):
    return np.asarray(x, np.float32).astype(ml_dtypes.bfloat16)


def planes(Y):
    r, m = Y.shape
    b = f64(bf(Y)).reshape(r // 32, 32, m)
    amax = np.abs(b).max(1)
    byte = np.clip(np.where(amax > 0, np.frexp(amax)[1] - 1 + 127 - 7, 1), 1, 254)
    codes = (b * np.exp2(127.0 - byte)[:, None, :]).reshape(r, m).astype(np.float32).astype(ml_dtypes.float8_e4m3fn).view(np.uint8)
    words = codes.reshape(r // 512, 128, 4, m).transpose(0, 1, 3, 2)
    return np.ascontiguousarray(words), np.ascontiguousarray(byte.astype(np.uint8).reshape(r // 512, 16, m))


K, T, J, R, V, N, C = 1024, 512, 128, 512, 512, 512, 1024


def setup_inputs():
    n = np.random.standard_normal
    idx = np.random.permutation(T)[:J]
    idx2 = np.random.permutation(V)[:J]
    idx3 = np.random.permutation(C)[:J]
    fk = mx_kscale(K)
    fr = mx_kscale(R)
    xtp = pack_weight(n((K, T)) / fk[:, None], "e5m2")
    wp = pack_weight(n((K, R)) * 1 / np.sqrt(K) * fk[:, None] * fr, "e4m3")
    wbp = pack_weight(n((R, N)) * 1 / np.sqrt(R) / fr[:, None], "e2m1")
    return {
        "xt_words": xtp[0],
        "xt_scales": xtp[1],
        "w_words": wp[0],
        "w_scales": wp[1],
        "tb": (n((R, V)) * 0.7).astype(np.float32),
        "wb_words": wbp[0],
        "wb_scales": wbp[1],
        "old": (1.0 * n((N, C))).astype(np.float32),
        "offs": striped(idx),
        "offs2": striped(idx2),
        "offs3": striped(idx3),
    }


def reference(xt_words, xt_scales, w_words, w_scales, tb, wb_words, wb_scales, old, offs, offs2, offs3):
    idx = unstriped(offs)
    idx2 = unstriped(offs2)
    idx3 = unstriped(offs3)
    xtu = unpack_weight(xt_words, xt_scales, "e5m2")
    wu = unpack_weight(w_words, w_scales, "e4m3")
    wbu = unpack_weight(wb_words, wb_scales, "e2m1")
    xtidxg = xtu[:, idx]
    a = wu.T @ xtidxg
    hid = np.maximum(a, 0.0) * f64(tb)[:, idx2]
    hidq = mxq(hid, 0, "e5m2")
    p = wbu.T @ hidq
    pp = np.zeros((N, C))
    pp[:, idx3] = p
    y = pp + 0.5 * f64(old)
    words, scales = planes(y)
    return y, words, scales

@@ -1,0 +1,224 @@
+from contextlib import ExitStack
+
+import concourse.mybir as mybir
+
+K, T, J, R, V, N, C = 1024, 512, 128, 512, 512, 512, 1024
+FLOPS = 2 * J * (K * R + R * N)
+
+F32 = mybir.dt.float32
+BF16 = mybir.dt.bfloat16
+I32 = mybir.dt.int32
+U32 = mybir.dt.uint32
+U16 = mybir.dt.uint16
+U8 = mybir.dt.uint8
+E4M3 = mybir.dt.float8_e4m3fn_x4
+E5M2 = mybir.dt.float8_e5m2_x4
+E2M1 = mybir.dt.float4_e2m1fn_x4
+ALU = mybir.AluOpType
+COPY = mybir.ActivationFunctionType.Copy
+
+P = 128
+PACK = 4
+PASSES = K // (P * PACK)
+CHUNK = 256
+OLD_W = 512
+
+
+def tile_list_picked_timestable_scattered_pl_kernel(
+    tc, xt_words, xt_scales, w_words, w_scales, tb, wb_words, wb_scales, old, offs, offs2, offs3, out_0, out_1, out_2
+):
+    nc = tc.nc
+    with ExitStack() as ctx:
+        sb = ctx.enter_context(tc.tile_pool(name="sb", bufs=1))
+        reuse = ctx.enter_context(tc.tile_pool(name="reuse", bufs=1))
+        ps = ctx.enter_context(tc.psum_pool(name="ps", bufs=1))
+
+        def load_scale_rows(queue, plane, rows):
+            for q in range(4):
+                queue.dma_start(
+                    out=plane[32 * q : 32 * q + 4, :, :].bitcast(I32),
+                    in_=rows[:, 4 * q : 4 * q + 4, :].rearrange("z r c -> r z c").bitcast(I32),
+                )
+
+        list_x = sb.tile([P, J // 16], U16, name="list_x")
+        list_tb = sb.tile([P, J // 16], U16, name="list_tb")
+        list_page = sb.tile([P, J // 16], U16, name="list_page")
+        xs = sb.tile([P, PASSES, T], U8, name="xs")
+        ws = sb.tile([P, PASSES, R], U8, name="ws")
+        bs = sb.tile([P, 1, N], U8, name="bs")
+        xw = sb.tile([P, PASSES, T], I32, name="xw")
+        ww = reuse.tile([P, PASSES, R], I32, name="ww", offset=0, align_bytes=64)
+        bw = sb.tile([P, 2 * N], U8, name="bw")
+        tbs = [sb.tile([P, 2, V], F32, name="tb%d" % h) for h in range(2)]
+        olds = [sb.tile([P, PACK, OLD_W], F32, name="old%d" % h) for h in range(C // OLD_W)]
+        pages = [sb.tile([P, C], F32, name="page%d" % t) for t in range(PACK)]
+
+        nc.vector.memset(xs[:].bitcast(I32), 0)
+        nc.vector.memset(ws[:].bitcast(I32), 0)
+        nc.gpsimd.memset(bs[:].bitcast(I32), 0)
+        for t in range(PACK):
+            nc.vector.memset(pages[t][:].bitcast(I32), 0)
+
+        nc.sync.dma_start(list_x[:], offs)
+        load_scale_rows(nc.scalar, xs, xt_scales)
+        nc.sync.dma_start(out=xw[:], in_=xt_words.rearrange("z p c b -> p z (c b)").bitcast(I32))
+        nc.sync.dma_start(out=ww[:], in_=w_words.rearrange("z p c b -> p z (c b)").bitcast(I32))
+        load_scale_rows(nc.scalar, ws, w_scales)
+        load_scale_rows(nc.gpsimd, bs, wb_scales)
+        nc.sync.dma_start(list_tb[:], offs2)
+        nc.scalar.dma_start(out=bw[:].bitcast(I32), in_=wb_words[0].bitcast(I32))
+        tb_rows = tb.rearrange("(p t) v -> p t v", t=PACK)
+        for h in range(2):
+            nc.sync.dma_start(out=tbs[h][:], in_=tb_rows[:, 2 * h : 2 * h + 2, :])
+        nc.sync.dma_start(list_page[:], offs3)
+        old_rows = old.rearrange("(p t) c -> p t c", t=PACK)
+        for h in range(C // OLD_W):
+            nc.sync.dma_start(out=olds[h][:], in_=old_rows[:, :, h * OLD_W : (h + 1) * OLD_W])
+
+        xg = sb.tile([P, PASSES, J], U32, name="xg", align_bytes=64)
+        xsg = sb.tile([P, PASSES, J], U8, name="xsg", align_bytes=64)
+        for z in range(PASSES):
+            nc.vector.tensor_copy(xsg[:, z, :], xs[:, z, :].indirect(list_x[:]))
+        for z in range(PASSES):
+            nc.vector.tensor_copy(xg[:, z, :], xw[:, z, :].bitcast(U32).indirect(list_x[:]))
+
+        wd = sb.tile([P, PASSES, R], I32, name="wd", align_bytes=64)
+        wsd = sb.tile([P, PASSES, R], U8, name="wsd", align_bytes=64)
+        a_ps = ps.tile([P, PACK, J], F32, name="a_ps")
+        for z in range(PASSES):
+            nc.vector.tensor_copy(
+                wd[:, z, :].rearrange("p (t m i) -> p m t i", t=PACK, i=4),
+                ww[:, z, :].rearrange("p (m i t) -> p m t i", t=PACK, i=4),
+            )
+            nc.vector.tensor_copy(
+                wsd[:, z, :].rearrange("p (t m) -> p t m", t=PACK),
+                ws[:, z, :].rearrange("p (m t) -> p t m", t=PACK),
+            )
+            for t in range(PACK):
+                cols = slice(t * P, (t + 1) * P)
+                nc.tensor.matmul_mx(
+                    out=a_ps[:, t, :],
+                    lhsT=wd[:, z, cols].bitcast(E4M3),
+                    lhsT_scale=wsd[:, z, cols],
+                    rhs=xg[:, z, :].bitcast(E5M2),
+                    rhs_scale=xsg[:, z, :],
+                    start=(z == 0 and t == 0),
+                    stop=(z == PASSES - 1 and t == PACK - 1),
+                )
+
+        bd = reuse.tile([P, 2 * N], U8, name="bd", offset=0, align_bytes=64)
+        bsd = sb.tile([P, N], U8, name="bsd", align_bytes=64)
+        nc.vector.tensor_copy(
+            bd[:].bitcast(U16).rearrange("p (t m) -> p t m", t=PACK),
+            bw[:].bitcast(U16).rearrange("p (m t) -> p t m", t=PACK),
+        )
+        nc.gpsimd.tensor_copy(
+            bsd[:].rearrange("p (t m) -> p t m", t=PACK),
+            bs[:, 0, :].rearrange("p (m t) -> p t m", t=PACK),
+        )
+
+        tg = sb.tile([P, PACK, J], F32, name="tg")
+        for t in range(PACK):
+            window = tbs[t // 2][:, t % 2, :].indirect(list_tb[:])
+            if t < PACK - 1:
+                nc.scalar.activation(tg[:, t, :], window, COPY)
+            else:
+                nc.vector.tensor_copy(tg[:, t, :], window)
+
+        hid = sb.tile([P, J, PACK], BF16, name="hid", align_bytes=64)
+        nc.vector.scalar_tensor_tensor(
+            out=hid[:],
+            in0=a_ps[:].rearrange("p t j -> p j t"),
+            scalar=0.0,
+            in1=tg[:].rearrange("p t j -> p j t"),
+            op0=ALU.max,
+            op1=ALU.mult,
+        )
+        hq = sb.tile([P, J], U32, name="hq", align_bytes=64)
+        hs = sb.tile([P, J], U8, name="hs", align_bytes=64)
+        nc.vector.quantize_mx(out=hq[:].bitcast(E5M2), scales=hs[:], in_=hid[:].rearrange("p j t -> p (j t)"))
+
+        p0_ps = ps.tile([P, J], F32, name="p0_ps")
+        p1_ps = ps.tile([P, J], F32, name="p1_ps")
+        p23_ps = ps.tile([P, 2, J], F32, name="p23_ps")
+        p_ps = [p0_ps[:], p1_ps[:], p23_ps[:, 0, :], p23_ps[:, 1, :]]
+        for t in (1, 0, 2, 3):
+            nc.tensor.matmul_mx(
+                out=p_ps[t],
+                lhsT=bd[:, 2 * t * P : 2 * (t + 1) * P].bitcast(E2M1),
+                lhsT_scale=bsd[:, t * P : (t + 1) * P],
+                rhs=hq[:].bitcast(E5M2),
+                rhs_scale=hs[:],
+                start=True,
+                stop=True,
+            )
+
+        p0 = sb.tile([P, J], F32, name="p0")
+        p1 = sb.tile([P, J], F32, name="p1")
+        p23 = sb.tile([P, 2, J], F32, name="p23")
+        nc.scalar.copy(p1[:], p1_ps[:])
+        nc.vector.tensor_copy(p0[:], p0_ps[:])
+        nc.scalar.copy(p23[:], p23_ps[:])
+        nc.vector.tensor_copy(pages[0][:].indirect(list_page[:]), p0[:])
+        nc.scalar.activation(pages[1][:].indirect(list_page[:]), p1[:], COPY)
+        for t in (2, 3):
+            nc.scalar.activation(pages[t][:].indirect(list_page[:]), p23[:, t - 2, :], COPY)
+
+        y_rows = out_0.rearrange("(p t) c -> p t c", t=PACK)
+        words_out = out_1[0].rearrange("p c b -> p (c b)").bitcast(I32)
+        ysc = sb.tile([P, C], U8, name="ysc", align_bytes=64)
+        y_first = sb.tile([P, PACK, OLD_W], F32, name="y_first")
+        y_late = [sb.tile([P, PACK, CHUNK], F32, name="y_late%d" % n) for n in range(2)]
+        ys = [y_first[:, :, 0:CHUNK], y_first[:, :, CHUNK : 2 * CHUNK], y_late[0][:], y_late[1][:]]
+        ybs = [sb.tile([P, CHUNK * PACK], BF16, name="yb%d" % n, align_bytes=64) for n in range(4)]
+        yqs = [sb.tile([P, CHUNK], I32, name="yq%d" % n, align_bytes=64) for n in range(4)]
+
+        def add(dst, t, c0, width):
+            o0 = c0 % OLD_W
+            nc.vector.scalar_tensor_tensor(
+                out=dst,
+                in0=olds[c0 // OLD_W][:, t, o0 : o0 + width],
+                scalar=0.5,
+                in1=pages[t][:, c0 : c0 + width],
+                op0=ALU.mult,
+                op1=ALU.add,
+            )
+
+        def cast(copy, n, c0, c1):
+            copy(
+                ybs[n][:, PACK * c0 : PACK * c1].rearrange("p (c i t) -> p c t i", t=PACK, i=4),
+                ys[n][:, :, c0:c1].rearrange("p t (c i) -> p c t i", i=4),
+            )
+
+        def quantise(n):
+            cols = slice(n * CHUNK, (n + 1) * CHUNK)
+            nc.vector.quantize_mx(out=yqs[n][:].bitcast(E4M3), scales=ysc[:, cols], in_=ybs[n][:])
+            nc.sync.dma_start(out=words_out[:, cols], in_=yqs[n][:])
+
+        def late_chunk(n):
+            for t in range(PACK):
+                add(ys[n][:, t, :], t, n * CHUNK, CHUNK)
+            nc.sync.dma_start(out=y_rows[:, :, n * CHUNK : (n + 1) * CHUNK], in_=ys[n])
+
+        for t in range(PACK - 1):
+            add(y_first[:, t, :], t, 0, OLD_W)
+            nc.sync.dma_start(out=y_rows[:, t, 0:OLD_W], in_=y_first[:, t, :])
+        for n in range(2):
+            add(ys[n][:, PACK - 1, :], PACK - 1, n * CHUNK, CHUNK)
+            cast(nc.scalar.copy, n, 0, CHUNK)
+        nc.sync.dma_start(out=y_rows[:, PACK - 1, 0:OLD_W], in_=y_first[:, PACK - 1, :])
+        late_chunk(2)
+        cast(nc.scalar.copy, 2, 0, CHUNK)
+        quantise(0)
+        late_chunk(3)
+        cast(nc.scalar.copy, 3, 0, CHUNK // 2)
+        quantise(1)
+        cast(nc.vector.tensor_copy, 3, CHUNK // 2, CHUNK)
+        quantise(2)
+        quantise(3)
+        for q in range(4):
+            queue = nc.sync if q < 2 else nc.scalar
+            queue.dma_start(
+                out=out_2[0, 4 * q : 4 * q + 4, :].bitcast(I32),
+                in_=ysc[32 * q : 32 * q + 4, :].bitcast(I32),
+            )

@@ -33,12 +33,11 @@ def tile_list_picked_timestable_scattered_pl_kernel(
         reuse = ctx.enter_context(tc.tile_pool(name="reuse", bufs=1))
         ps = ctx.enter_context(tc.psum_pool(name="ps", bufs=1))
 
-        def load_scale_rows(queue, plane, rows):
-            for q in range(4):
-                queue.dma_start(
-                    out=plane[32 * q : 32 * q + 4, :, :].bitcast(I32),
-                    in_=rows[:, 4 * q : 4 * q + 4, :].rearrange("z r c -> r z c").bitcast(I32),
-                )
+        def load_scale_rows(plane, rows, q):
+            nc.sync.dma_start(
+                out=plane[32 * q : 32 * q + 4, :, :].bitcast(I32),
+                in_=rows[:, 4 * q : 4 * q + 4, :].rearrange("z r c -> r z c").bitcast(I32),
+            )
 
         list_x = sb.tile([P, J // 16], U16, name="list_x")
         list_tb = sb.tile([P, J // 16], U16, name="list_tb")
@@ -47,8 +46,8 @@ def tile_list_picked_timestable_scattered_pl_kernel(
         ws = sb.tile([P, PASSES, R], U8, name="ws")
         bs = sb.tile([P, 1, N], U8, name="bs")
         xw = sb.tile([P, PASSES, T], I32, name="xw")
-        ww = reuse.tile([P, PASSES, R], I32, name="ww", offset=0, align_bytes=64)
-        bw = sb.tile([P, 2 * N], U8, name="bw")
+        ww = sb.tile([P, PASSES, R], I32, name="ww")
+        bw = reuse.tile([P, 2 * N], U8, name="bw", tag="bw_hid", align_bytes=64)
         tbs = [sb.tile([P, 2, V], F32, name="tb%d" % h) for h in range(2)]
         olds = [sb.tile([P, PACK, OLD_W], F32, name="old%d" % h) for h in range(C // OLD_W)]
         pages = [sb.tile([P, C], F32, name="page%d" % t) for t in range(PACK)]
@@ -56,22 +55,27 @@ def tile_list_picked_timestable_scattered_pl_kernel(
         nc.vector.memset(xs[:].bitcast(I32), 0)
         nc.vector.memset(ws[:].bitcast(I32), 0)
         nc.gpsimd.memset(bs[:].bitcast(I32), 0)
-        for t in range(PACK):
+        for t in range(PACK - 1):
             nc.vector.memset(pages[t][:].bitcast(I32), 0)
+        nc.gpsimd.memset(pages[PACK - 1][:].bitcast(I32), 0)
 
-        nc.sync.dma_start(list_x[:], offs)
-        load_scale_rows(nc.scalar, xs, xt_scales)
-        nc.sync.dma_start(out=xw[:], in_=xt_words.rearrange("z p c b -> p z (c b)").bitcast(I32))
-        nc.sync.dma_start(out=ww[:], in_=w_words.rearrange("z p c b -> p z (c b)").bitcast(I32))
-        load_scale_rows(nc.scalar, ws, w_scales)
-        load_scale_rows(nc.gpsimd, bs, wb_scales)
-        nc.sync.dma_start(list_tb[:], offs2)
-        nc.scalar.dma_start(out=bw[:].bitcast(I32), in_=wb_words[0].bitcast(I32))
         tb_rows = tb.rearrange("(p t) v -> p t v", t=PACK)
-        for h in range(2):
-            nc.sync.dma_start(out=tbs[h][:], in_=tb_rows[:, 2 * h : 2 * h + 2, :])
-        nc.sync.dma_start(list_page[:], offs3)
         old_rows = old.rearrange("(p t) c -> p t c", t=PACK)
+        nc.sync.dma_start(list_x[:], offs)
+        nc.sync.dma_start(out=xw[:], in_=xt_words.rearrange("z p c b -> p z (c b)").bitcast(I32))
+        for q in range(4):
+            load_scale_rows(xs, xt_scales, q)
+        nc.sync.dma_start(out=ww[:], in_=w_words.rearrange("z p c b -> p z (c b)").bitcast(I32))
+        load_scale_rows(ws, w_scales, 0)
+        nc.sync.dma_start(out=tbs[0][:], in_=tb_rows[:, 0:2, :])
+        nc.sync.dma_start(list_tb[:], offs2)
+        for q in range(1, 4):
+            load_scale_rows(ws, w_scales, q)
+        nc.sync.dma_start(out=tbs[1][:], in_=tb_rows[:, 2:4, :])
+        nc.sync.dma_start(out=bw[:].bitcast(I32), in_=wb_words[0].bitcast(I32))
+        for q in range(4):
+            load_scale_rows(bs, wb_scales, q)
+        nc.sync.dma_start(list_page[:], offs3)
         for h in range(C // OLD_W):
             nc.sync.dma_start(out=olds[h][:], in_=old_rows[:, :, h * OLD_W : (h + 1) * OLD_W])
 
@@ -90,10 +94,12 @@ def tile_list_picked_timestable_scattered_pl_kernel(
                 wd[:, z, :].rearrange("p (t m i) -> p m t i", t=PACK, i=4),
                 ww[:, z, :].rearrange("p (m i t) -> p m t i", t=PACK, i=4),
             )
-            nc.vector.tensor_copy(
-                wsd[:, z, :].rearrange("p (t m) -> p t m", t=PACK),
-                ws[:, z, :].rearrange("p (m t) -> p t m", t=PACK),
-            )
+        for z in range(PASSES):
+            for slots in ([slice(0, 1), slice(1, PACK)] if z == 0 else [slice(0, PACK)]):
+                nc.vector.tensor_copy(
+                    wsd[:, z, :].rearrange("p (t m) -> p t m", t=PACK)[:, slots, :],
+                    ws[:, z, :].rearrange("p (m t) -> p t m", t=PACK)[:, slots, :],
+                )
             for t in range(PACK):
                 cols = slice(t * P, (t + 1) * P)
                 nc.tensor.matmul_mx(
@@ -106,7 +112,7 @@ def tile_list_picked_timestable_scattered_pl_kernel(
                     stop=(z == PASSES - 1 and t == PACK - 1),
                 )
 
-        bd = reuse.tile([P, 2 * N], U8, name="bd", offset=0, align_bytes=64)
+        bd = sb.tile([P, 2 * N], U8, name="bd", align_bytes=64)
         bsd = sb.tile([P, N], U8, name="bsd", align_bytes=64)
         nc.vector.tensor_copy(
             bd[:].bitcast(U16).rearrange("p (t m) -> p t m", t=PACK),
@@ -125,18 +131,23 @@ def tile_list_picked_timestable_scattered_pl_kernel(
             else:
                 nc.vector.tensor_copy(tg[:, t, :], window)
 
-        hid = sb.tile([P, J, PACK], BF16, name="hid", align_bytes=64)
-        nc.vector.scalar_tensor_tensor(
-            out=hid[:],
-            in0=a_ps[:].rearrange("p t j -> p j t"),
-            scalar=0.0,
-            in1=tg[:].rearrange("p t j -> p j t"),
-            op0=ALU.max,
-            op1=ALU.mult,
-        )
+        hid = reuse.tile([P, J, PACK], BF16, name="hid", tag="bw_hid", align_bytes=64)
         hq = sb.tile([P, J], U32, name="hq", align_bytes=64)
         hs = sb.tile([P, J], U8, name="hs", align_bytes=64)
-        nc.vector.quantize_mx(out=hq[:].bitcast(E5M2), scales=hs[:], in_=hid[:].rearrange("p j t -> p (j t)"))
+        halves = [slice(0, J // 2), slice(J // 2, J)]
+        for js in halves:
+            nc.vector.scalar_tensor_tensor(
+                out=hid[:, js, :],
+                in0=a_ps[:, :, js].rearrange("p t j -> p j t"),
+                scalar=0.0,
+                in1=tg[:, :, js].rearrange("p t j -> p j t"),
+                op0=ALU.max,
+                op1=ALU.mult,
+            )
+        for js in halves:
+            nc.vector.quantize_mx(
+                out=hq[:, js].bitcast(E5M2), scales=hs[:, js], in_=hid[:, js, :].rearrange("p j t -> p (j t)")
+            )
 
         p0_ps = ps.tile([P, J], F32, name="p0_ps")
         p1_ps = ps.tile([P, J], F32, name="p1_ps")
@@ -158,7 +169,7 @@ def tile_list_picked_timestable_scattered_pl_kernel(
         p23 = sb.tile([P, 2, J], F32, name="p23")
         nc.scalar.copy(p1[:], p1_ps[:])
         nc.vector.tensor_copy(p0[:], p0_ps[:])
-        nc.scalar.copy(p23[:], p23_ps[:])
+        nc.vector.tensor_copy(p23[:], p23_ps[:])
         nc.vector.tensor_copy(pages[0][:].indirect(list_page[:]), p0[:])
         nc.scalar.activation(pages[1][:].indirect(list_page[:]), p1[:], COPY)
         for t in (2, 3):
@@ -190,10 +201,15 @@ def tile_list_picked_timestable_scattered_pl_kernel(
                 ys[n][:, :, c0:c1].rearrange("p t (c i) -> p c t i", i=4),
             )
 
-        def quantise(n):
-            cols = slice(n * CHUNK, (n + 1) * CHUNK)
-            nc.vector.quantize_mx(out=yqs[n][:].bitcast(E4M3), scales=ysc[:, cols], in_=ybs[n][:])
-            nc.sync.dma_start(out=words_out[:, cols], in_=yqs[n][:])
+        def quantise(n, c0, c1):
+            nc.vector.quantize_mx(
+                out=yqs[n][:, c0:c1].bitcast(E4M3),
+                scales=ysc[:, n * CHUNK + c0 : n * CHUNK + c1],
+                in_=ybs[n][:, PACK * c0 : PACK * c1],
+            )
+
+        def store_words(n):
+            nc.sync.dma_start(out=words_out[:, n * CHUNK : (n + 1) * CHUNK], in_=yqs[n][:])
 
         def late_chunk(n):
             for t in range(PACK):
@@ -209,13 +225,18 @@ def tile_list_picked_timestable_scattered_pl_kernel(
         nc.sync.dma_start(out=y_rows[:, PACK - 1, 0:OLD_W], in_=y_first[:, PACK - 1, :])
         late_chunk(2)
         cast(nc.scalar.copy, 2, 0, CHUNK)
-        quantise(0)
+        quantise(0, 0, CHUNK)
+        store_words(0)
         late_chunk(3)
         cast(nc.scalar.copy, 3, 0, CHUNK // 2)
-        quantise(1)
+        quantise(1, 0, CHUNK)
+        store_words(1)
         cast(nc.vector.tensor_copy, 3, CHUNK // 2, CHUNK)
-        quantise(2)
-        quantise(3)
+        quantise(2, 0, CHUNK)
+        store_words(2)
+        quantise(3, CHUNK // 2, CHUNK)
+        quantise(3, 0, CHUNK // 2)
+        store_words(3)
         for q in range(4):
             queue = nc.sync if q < 2 else nc.scalar
             queue.dma_start(

@@ -21,7 +21,8 @@ P = 128
 PACK = 4
 PASSES = K // (P * PACK)
 CHUNK = 256
-OLD_W = 512
+HALF = C // 2
+OLD_PIECES = (slice(0, 1), slice(1, 3), slice(3, 5), slice(6, 7), slice(5, 8, 2))
 
 
 def tile_list_picked_timestable_scattered_pl_kernel(
@@ -49,18 +50,21 @@ def tile_list_picked_timestable_scattered_pl_kernel(
         ww = sb.tile([P, PASSES, R], I32, name="ww")
         bw = reuse.tile([P, 2 * N], U8, name="bw", tag="bw_hid", align_bytes=64)
         tbs = [sb.tile([P, 2, V], F32, name="tb%d" % h) for h in range(2)]
-        olds = [sb.tile([P, PACK, OLD_W], F32, name="old%d" % h) for h in range(C // OLD_W)]
-        pages = [sb.tile([P, C], F32, name="page%d" % t) for t in range(PACK)]
+        olds = [
+            sb.tile([P, len(range(8)[piece]), HALF], F32, name="old%d" % n) for n, piece in enumerate(OLD_PIECES)
+        ]
+        pages = [sb.tile([P, C], F32, name="page%d" % t) for t in range(PACK - 1)]
 
         nc.vector.memset(xs[:].bitcast(I32), 0)
         nc.vector.memset(ws[:].bitcast(I32), 0)
         nc.gpsimd.memset(bs[:].bitcast(I32), 0)
         for t in range(PACK - 1):
             nc.vector.memset(pages[t][:].bitcast(I32), 0)
-        nc.gpsimd.memset(pages[PACK - 1][:].bitcast(I32), 0)
+        warm = sb.tile([P, 8], F32, name="warm")
+        nc.scalar.activation(warm[:], pages[0][:, 0:8], COPY)
 
         tb_rows = tb.rearrange("(p t) v -> p t v", t=PACK)
-        old_rows = old.rearrange("(p t) c -> p t c", t=PACK)
+        old_halves = old.rearrange("(p t) (h c) -> p (t h) c", t=PACK, h=2)
         nc.sync.dma_start(list_x[:], offs)
         nc.sync.dma_start(out=xw[:], in_=xt_words.rearrange("z p c b -> p z (c b)").bitcast(I32))
         for q in range(4):
@@ -73,11 +77,13 @@ def tile_list_picked_timestable_scattered_pl_kernel(
             load_scale_rows(ws, w_scales, q)
         nc.sync.dma_start(out=tbs[1][:], in_=tb_rows[:, 2:4, :])
         nc.sync.dma_start(out=bw[:].bitcast(I32), in_=wb_words[0].bitcast(I32))
+        nc.sync.dma_start(out=olds[0][:], in_=old_halves[:, OLD_PIECES[0], :])
         for q in range(4):
             load_scale_rows(bs, wb_scales, q)
+        nc.sync.dma_start(out=olds[1][:], in_=old_halves[:, OLD_PIECES[1], :])
         nc.sync.dma_start(list_page[:], offs3)
-        for h in range(C // OLD_W):
-            nc.sync.dma_start(out=olds[h][:], in_=old_rows[:, :, h * OLD_W : (h + 1) * OLD_W])
+        for n in range(2, len(OLD_PIECES)):
+            nc.sync.dma_start(out=olds[n][:], in_=old_halves[:, OLD_PIECES[n], :])
 
         xg = sb.tile([P, PASSES, J], U32, name="xg", align_bytes=64)
         xsg = sb.tile([P, PASSES, J], U8, name="xsg", align_bytes=64)
@@ -150,12 +156,10 @@ def tile_list_picked_timestable_scattered_pl_kernel(
             )
 
         p0_ps = ps.tile([P, J], F32, name="p0_ps")
-        p1_ps = ps.tile([P, J], F32, name="p1_ps")
-        p23_ps = ps.tile([P, 2, J], F32, name="p23_ps")
-        p_ps = [p0_ps[:], p1_ps[:], p23_ps[:, 0, :], p23_ps[:, 1, :]]
-        for t in (1, 0, 2, 3):
+        rest_ps = ps.tile([P, PACK - 1, J], F32, name="rest_ps")
+        for t in range(PACK):
             nc.tensor.matmul_mx(
-                out=p_ps[t],
+                out=p0_ps[:] if t == 0 else rest_ps[:, t - 1, :],
                 lhsT=bd[:, 2 * t * P : 2 * (t + 1) * P].bitcast(E2M1),
                 lhsT_scale=bsd[:, t * P : (t + 1) * P],
                 rhs=hq[:].bitcast(E5M2),
@@ -165,78 +169,76 @@ def tile_list_picked_timestable_scattered_pl_kernel(
             )
 
         p0 = sb.tile([P, J], F32, name="p0")
-        p1 = sb.tile([P, J], F32, name="p1")
-        p23 = sb.tile([P, 2, J], F32, name="p23")
-        nc.scalar.copy(p1[:], p1_ps[:])
+        rest = sb.tile([P, PACK - 1, J], F32, name="rest")
         nc.vector.tensor_copy(p0[:], p0_ps[:])
-        nc.vector.tensor_copy(p23[:], p23_ps[:])
+        nc.scalar.copy(rest[:], rest_ps[:])
         nc.vector.tensor_copy(pages[0][:].indirect(list_page[:]), p0[:])
-        nc.scalar.activation(pages[1][:].indirect(list_page[:]), p1[:], COPY)
-        for t in (2, 3):
-            nc.scalar.activation(pages[t][:].indirect(list_page[:]), p23[:, t - 2, :], COPY)
+        for t in (1, 2):
+            nc.scalar.activation(pages[t][:].indirect(list_page[:]), rest[:, t - 1, :], COPY)
+        page_of = [pages[0], pages[1], pages[2], pages[0]]
 
         y_rows = out_0.rearrange("(p t) c -> p t c", t=PACK)
         words_out = out_1[0].rearrange("p c b -> p (c b)").bitcast(I32)
         ysc = sb.tile([P, C], U8, name="ysc", align_bytes=64)
-        y_first = sb.tile([P, PACK, OLD_W], F32, name="y_first")
-        y_late = [sb.tile([P, PACK, CHUNK], F32, name="y_late%d" % n) for n in range(2)]
-        ys = [y_first[:, :, 0:CHUNK], y_first[:, :, CHUNK : 2 * CHUNK], y_late[0][:], y_late[1][:]]
+        yq = sb.tile([P, C], I32, name="yq", align_bytes=64)
+        ys = [sb.tile([P, PACK, HALF], F32, name="y%d" % h) for h in range(2)]
         ybs = [sb.tile([P, CHUNK * PACK], BF16, name="yb%d" % n, align_bytes=64) for n in range(4)]
-        yqs = [sb.tile([P, CHUNK], I32, name="yq%d" % n, align_bytes=64) for n in range(4)]
 
-        def add(dst, t, c0, width):
-            o0 = c0 % OLD_W
+        old_half = {}
+        for n, piece in enumerate(OLD_PIECES):
+            for place, u in enumerate(range(8)[piece]):
+                old_half[u] = olds[n][:, place, :]
+
+        def add(t, c0, width):
             nc.vector.scalar_tensor_tensor(
-                out=dst,
-                in0=olds[c0 // OLD_W][:, t, o0 : o0 + width],
+                out=ys[c0 // HALF][:, t, c0 % HALF : c0 % HALF + width],
+                in0=old_half[2 * t + c0 // HALF][:, c0 % HALF : c0 % HALF + width],
                 scalar=0.5,
-                in1=pages[t][:, c0 : c0 + width],
+                in1=page_of[t][:, c0 : c0 + width],
                 op0=ALU.mult,
                 op1=ALU.add,
             )
 
+        def store_y(slots, h):
+            nc.sync.dma_start(out=y_rows[:, slots, h * HALF : (h + 1) * HALF], in_=ys[h][:, slots, :])
+
         def cast(copy, n, c0, c1):
+            base = n * CHUNK % HALF
             copy(
                 ybs[n][:, PACK * c0 : PACK * c1].rearrange("p (c i t) -> p c t i", t=PACK, i=4),
-                ys[n][:, :, c0:c1].rearrange("p t (c i) -> p c t i", i=4),
+                ys[n * CHUNK // HALF][:, :, base + c0 : base + c1].rearrange("p t (c i) -> p c t i", i=4),
             )
 
         def quantise(n, c0, c1):
+            cols = slice(n * CHUNK + c0, n * CHUNK + c1)
             nc.vector.quantize_mx(
-                out=yqs[n][:, c0:c1].bitcast(E4M3),
-                scales=ysc[:, n * CHUNK + c0 : n * CHUNK + c1],
-                in_=ybs[n][:, PACK * c0 : PACK * c1],
+                out=yq[:, cols].bitcast(E4M3), scales=ysc[:, cols], in_=ybs[n][:, PACK * c0 : PACK * c1]
             )
 
-        def store_words(n):
-            nc.sync.dma_start(out=words_out[:, n * CHUNK : (n + 1) * CHUNK], in_=yqs[n][:])
+        def store_words(c0, c1):
+            nc.sync.dma_start(out=words_out[:, c0:c1], in_=yq[:, c0:c1])
 
-        def late_chunk(n):
-            for t in range(PACK):
-                add(ys[n][:, t, :], t, n * CHUNK, CHUNK)
-            nc.sync.dma_start(out=y_rows[:, :, n * CHUNK : (n + 1) * CHUNK], in_=ys[n])
-
-        for t in range(PACK - 1):
-            add(y_first[:, t, :], t, 0, OLD_W)
-            nc.sync.dma_start(out=y_rows[:, t, 0:OLD_W], in_=y_first[:, t, :])
-        for n in range(2):
-            add(ys[n][:, PACK - 1, :], PACK - 1, n * CHUNK, CHUNK)
+        for h in range(2):
+            add(0, h * HALF, HALF)
+            store_y(slice(0, 1), h)
+        nc.scalar.activation(pages[0][:].indirect(list_page[:]), rest[:, 2, :], COPY)
+        for h in range(2):
+            add(1, h * HALF, HALF)
+            store_y(slice(1, 2), h)
+            for t in (2, 3):
+                for n in (2 * h, 2 * h + 1):
+                    add(t, n * CHUNK, CHUNK)
+            store_y(slice(2, 4), h)
+        for n in range(3):
             cast(nc.scalar.copy, n, 0, CHUNK)
-        nc.sync.dma_start(out=y_rows[:, PACK - 1, 0:OLD_W], in_=y_first[:, PACK - 1, :])
-        late_chunk(2)
-        cast(nc.scalar.copy, 2, 0, CHUNK)
         quantise(0, 0, CHUNK)
-        store_words(0)
-        late_chunk(3)
-        cast(nc.scalar.copy, 3, 0, CHUNK // 2)
+        cast(nc.vector.tensor_copy, 3, 0, CHUNK)
         quantise(1, 0, CHUNK)
-        store_words(1)
-        cast(nc.vector.tensor_copy, 3, CHUNK // 2, CHUNK)
+        store_words(0, HALF)
+        quantise(3, 0, CHUNK)
+        store_words(3 * CHUNK, 4 * CHUNK)
         quantise(2, 0, CHUNK)
-        store_words(2)
-        quantise(3, CHUNK // 2, CHUNK)
-        quantise(3, 0, CHUNK // 2)
-        store_words(3)
+        store_words(2 * CHUNK, 3 * CHUNK)
         for q in range(4):
             queue = nc.sync if q < 2 else nc.scalar
             queue.dma_start(

@@ -21,6 +21,7 @@ P = 128
 PACK = 4
 PASSES = K // (P * PACK)
 CHUNK = 256
+SCALAR_SHARE = 192
 HALF = C // 2
 OLD_PIECES = (slice(0, 1), slice(1, 3), slice(3, 5), slice(6, 7), slice(5, 8, 2))
 
@@ -205,8 +206,8 @@ def tile_list_picked_timestable_scattered_pl_kernel(
         def cast(copy, n, c0, c1):
             base = n * CHUNK % HALF
             copy(
-                ybs[n][:, PACK * c0 : PACK * c1].rearrange("p (c i t) -> p c t i", t=PACK, i=4),
-                ys[n * CHUNK // HALF][:, :, base + c0 : base + c1].rearrange("p t (c i) -> p c t i", i=4),
+                ybs[n][:, PACK * c0 : PACK * c1].rearrange("p (c i t) -> p c t i", t=PACK, i=2),
+                ys[n * CHUNK // HALF][:, :, base + c0 : base + c1].rearrange("p t (c i) -> p c t i", i=2),
             )
 
         def quantise(n, c0, c1):
@@ -229,10 +230,12 @@ def tile_list_picked_timestable_scattered_pl_kernel(
                 for n in (2 * h, 2 * h + 1):
                     add(t, n * CHUNK, CHUNK)
             store_y(slice(2, 4), h)
-        for n in range(3):
-            cast(nc.scalar.copy, n, 0, CHUNK)
+        cast(nc.scalar.copy, 0, 0, CHUNK)
+        cast(nc.scalar.copy, 1, 0, CHUNK)
+        cast(nc.scalar.copy, 2, 0, SCALAR_SHARE)
         quantise(0, 0, CHUNK)
         cast(nc.vector.tensor_copy, 3, 0, CHUNK)
+        cast(nc.vector.tensor_copy, 2, SCALAR_SHARE, CHUNK)
         quantise(1, 0, CHUNK)
         store_words(0, HALF)
         quantise(3, 0, CHUNK)

from contextlib import ExitStack

import concourse.mybir as mybir

K, T, J, R, V, N, C = 1024, 512, 128, 512, 512, 512, 1024
FLOPS = 2 * J * (K * R + R * N)

F32 = mybir.dt.float32
BF16 = mybir.dt.bfloat16
I32 = mybir.dt.int32
U32 = mybir.dt.uint32
U16 = mybir.dt.uint16
U8 = mybir.dt.uint8
E4M3 = mybir.dt.float8_e4m3fn_x4
E5M2 = mybir.dt.float8_e5m2_x4
E2M1 = mybir.dt.float4_e2m1fn_x4
ALU = mybir.AluOpType
COPY = mybir.ActivationFunctionType.Copy

P = 128
PACK = 4
PASSES = K // (P * PACK)
CHUNK = 256
SCALAR_SHARE = 192
HALF = C // 2
OLD_PIECES = (slice(0, 1), slice(1, 3), slice(3, 5), slice(6, 7), slice(5, 8, 2))


def tile_list_picked_timestable_scattered_pl_kernel(
    tc, xt_words, xt_scales, w_words, w_scales, tb, wb_words, wb_scales, old, offs, offs2, offs3, out_0, out_1, out_2
):
    nc = tc.nc
    with ExitStack() as ctx:
        sb = ctx.enter_context(tc.tile_pool(name="sb", bufs=1))
        reuse = ctx.enter_context(tc.tile_pool(name="reuse", bufs=1))
        ps = ctx.enter_context(tc.psum_pool(name="ps", bufs=1))

        def load_scale_rows(plane, rows, q):
            nc.sync.dma_start(
                out=plane[32 * q : 32 * q + 4, :, :].bitcast(I32),
                in_=rows[:, 4 * q : 4 * q + 4, :].rearrange("z r c -> r z c").bitcast(I32),
            )

        list_x = sb.tile([P, J // 16], U16, name="list_x")
        list_tb = sb.tile([P, J // 16], U16, name="list_tb")
        list_page = sb.tile([P, J // 16], U16, name="list_page")
        xs = sb.tile([P, PASSES, T], U8, name="xs")
        ws = sb.tile([P, PASSES, R], U8, name="ws")
        bs = sb.tile([P, 1, N], U8, name="bs")
        xw = sb.tile([P, PASSES, T], I32, name="xw")
        ww = sb.tile([P, PASSES, R], I32, name="ww")
        bw = reuse.tile([P, 2 * N], U8, name="bw", tag="bw_hid", align_bytes=64)
        tbs = [sb.tile([P, 2, V], F32, name="tb%d" % h) for h in range(2)]
        olds = [
            sb.tile([P, len(range(8)[piece]), HALF], F32, name="old%d" % n) for n, piece in enumerate(OLD_PIECES)
        ]
        pages = [sb.tile([P, C], F32, name="page%d" % t) for t in range(PACK - 1)]

        nc.vector.memset(xs[:].bitcast(I32), 0)
        nc.vector.memset(ws[:].bitcast(I32), 0)
        nc.gpsimd.memset(bs[:].bitcast(I32), 0)
        for t in range(PACK - 1):
            nc.vector.memset(pages[t][:].bitcast(I32), 0)
        warm = sb.tile([P, 8], F32, name="warm")
        nc.scalar.activation(warm[:], pages[0][:, 0:8], COPY)

        tb_rows = tb.rearrange("(p t) v -> p t v", t=PACK)
        old_halves = old.rearrange("(p t) (h c) -> p (t h) c", t=PACK, h=2)
        nc.sync.dma_start(list_x[:], offs)
        nc.sync.dma_start(out=xw[:], in_=xt_words.rearrange("z p c b -> p z (c b)").bitcast(I32))
        for q in range(4):
            load_scale_rows(xs, xt_scales, q)
        nc.sync.dma_start(out=ww[:], in_=w_words.rearrange("z p c b -> p z (c b)").bitcast(I32))
        load_scale_rows(ws, w_scales, 0)
        nc.sync.dma_start(out=tbs[0][:], in_=tb_rows[:, 0:2, :])
        nc.sync.dma_start(list_tb[:], offs2)
        for q in range(1, 4):
            load_scale_rows(ws, w_scales, q)
        nc.sync.dma_start(out=tbs[1][:], in_=tb_rows[:, 2:4, :])
        nc.sync.dma_start(out=bw[:].bitcast(I32), in_=wb_words[0].bitcast(I32))
        nc.sync.dma_start(out=olds[0][:], in_=old_halves[:, OLD_PIECES[0], :])
        for q in range(4):
            load_scale_rows(bs, wb_scales, q)
        nc.sync.dma_start(out=olds[1][:], in_=old_halves[:, OLD_PIECES[1], :])
        nc.sync.dma_start(list_page[:], offs3)
        for n in range(2, len(OLD_PIECES)):
            nc.sync.dma_start(out=olds[n][:], in_=old_halves[:, OLD_PIECES[n], :])

        xg = sb.tile([P, PASSES, J], U32, name="xg", align_bytes=64)
        xsg = sb.tile([P, PASSES, J], U8, name="xsg", align_bytes=64)
        for z in range(PASSES):
            nc.vector.tensor_copy(xsg[:, z, :], xs[:, z, :].indirect(list_x[:]))
        for z in range(PASSES):
            nc.vector.tensor_copy(xg[:, z, :], xw[:, z, :].bitcast(U32).indirect(list_x[:]))

        wd = sb.tile([P, PASSES, R], I32, name="wd", align_bytes=64)
        wsd = sb.tile([P, PASSES, R], U8, name="wsd", align_bytes=64)
        a_ps = ps.tile([P, PACK, J], F32, name="a_ps")
        for z in range(PASSES):
            nc.vector.tensor_copy(
                wd[:, z, :].rearrange("p (t m i) -> p m t i", t=PACK, i=4),
                ww[:, z, :].rearrange("p (m i t) -> p m t i", t=PACK, i=4),
            )
        for z in range(PASSES):
            for slots in ([slice(0, 1), slice(1, PACK)] if z == 0 else [slice(0, PACK)]):
                nc.vector.tensor_copy(
                    wsd[:, z, :].rearrange("p (t m) -> p t m", t=PACK)[:, slots, :],
                    ws[:, z, :].rearrange("p (m t) -> p t m", t=PACK)[:, slots, :],
                )
            for t in range(PACK):
                cols = slice(t * P, (t + 1) * P)
                nc.tensor.matmul_mx(
                    out=a_ps[:, t, :],
                    lhsT=wd[:, z, cols].bitcast(E4M3),
                    lhsT_scale=wsd[:, z, cols],
                    rhs=xg[:, z, :].bitcast(E5M2),
                    rhs_scale=xsg[:, z, :],
                    start=(z == 0 and t == 0),
                    stop=(z == PASSES - 1 and t == PACK - 1),
                )

        bd = sb.tile([P, 2 * N], U8, name="bd", align_bytes=64)
        bsd = sb.tile([P, N], U8, name="bsd", align_bytes=64)
        nc.vector.tensor_copy(
            bd[:].bitcast(U16).rearrange("p (t m) -> p t m", t=PACK),
            bw[:].bitcast(U16).rearrange("p (m t) -> p t m", t=PACK),
        )
        nc.gpsimd.tensor_copy(
            bsd[:].rearrange("p (t m) -> p t m", t=PACK),
            bs[:, 0, :].rearrange("p (m t) -> p t m", t=PACK),
        )

        tg = sb.tile([P, PACK, J], F32, name="tg")
        for t in range(PACK):
            window = tbs[t // 2][:, t % 2, :].indirect(list_tb[:])
            if t < PACK - 1:
                nc.scalar.activation(tg[:, t, :], window, COPY)
            else:
                nc.vector.tensor_copy(tg[:, t, :], window)

        hid = reuse.tile([P, J, PACK], BF16, name="hid", tag="bw_hid", align_bytes=64)
        hq = sb.tile([P, J], U32, name="hq", align_bytes=64)
        hs = sb.tile([P, J], U8, name="hs", align_bytes=64)
        halves = [slice(0, J // 2), slice(J // 2, J)]
        for js in halves:
            nc.vector.scalar_tensor_tensor(
                out=hid[:, js, :],
                in0=a_ps[:, :, js].rearrange("p t j -> p j t"),
                scalar=0.0,
                in1=tg[:, :, js].rearrange("p t j -> p j t"),
                op0=ALU.max,
                op1=ALU.mult,
            )
        for js in halves:
            nc.vector.quantize_mx(
                out=hq[:, js].bitcast(E5M2), scales=hs[:, js], in_=hid[:, js, :].rearrange("p j t -> p (j t)")
            )

        p0_ps = ps.tile([P, J], F32, name="p0_ps")
        rest_ps = ps.tile([P, PACK - 1, J], F32, name="rest_ps")
        for t in range(PACK):
            nc.tensor.matmul_mx(
                out=p0_ps[:] if t == 0 else rest_ps[:, t - 1, :],
                lhsT=bd[:, 2 * t * P : 2 * (t + 1) * P].bitcast(E2M1),
                lhsT_scale=bsd[:, t * P : (t + 1) * P],
                rhs=hq[:].bitcast(E5M2),
                rhs_scale=hs[:],
                start=True,
                stop=True,
            )

        p0 = sb.tile([P, J], F32, name="p0")
        rest = sb.tile([P, PACK - 1, J], F32, name="rest")
        nc.vector.tensor_copy(p0[:], p0_ps[:])
        nc.scalar.copy(rest[:], rest_ps[:])
        nc.vector.tensor_copy(pages[0][:].indirect(list_page[:]), p0[:])
        for t in (1, 2):
            nc.scalar.activation(pages[t][:].indirect(list_page[:]), rest[:, t - 1, :], COPY)
        page_of = [pages[0], pages[1], pages[2], pages[0]]

        y_rows = out_0.rearrange("(p t) c -> p t c", t=PACK)
        words_out = out_1[0].rearrange("p c b -> p (c b)").bitcast(I32)
        ysc = sb.tile([P, C], U8, name="ysc", align_bytes=64)
        yq = sb.tile([P, C], I32, name="yq", align_bytes=64)
        ys = [sb.tile([P, PACK, HALF], F32, name="y%d" % h) for h in range(2)]
        ybs = [sb.tile([P, CHUNK * PACK], BF16, name="yb%d" % n, align_bytes=64) for n in range(4)]

        old_half = {}
        for n, piece in enumerate(OLD_PIECES):
            for place, u in enumerate(range(8)[piece]):
                old_half[u] = olds[n][:, place, :]

        def add(t, c0, width):
            nc.vector.scalar_tensor_tensor(
                out=ys[c0 // HALF][:, t, c0 % HALF : c0 % HALF + width],
                in0=old_half[2 * t + c0 // HALF][:, c0 % HALF : c0 % HALF + width],
                scalar=0.5,
                in1=page_of[t][:, c0 : c0 + width],
                op0=ALU.mult,
                op1=ALU.add,
            )

        def store_y(slots, h):
            nc.sync.dma_start(out=y_rows[:, slots, h * HALF : (h + 1) * HALF], in_=ys[h][:, slots, :])

        def cast(copy, n, c0, c1):
            base = n * CHUNK % HALF
            copy(
                ybs[n][:, PACK * c0 : PACK * c1].rearrange("p (c i t) -> p c t i", t=PACK, i=2),
                ys[n * CHUNK // HALF][:, :, base + c0 : base + c1].rearrange("p t (c i) -> p c t i", i=2),
            )

        def quantise(n, c0, c1):
            cols = slice(n * CHUNK + c0, n * CHUNK + c1)
            nc.vector.quantize_mx(
                out=yq[:, cols].bitcast(E4M3), scales=ysc[:, cols], in_=ybs[n][:, PACK * c0 : PACK * c1]
            )

        def store_words(c0, c1):
            nc.sync.dma_start(out=words_out[:, c0:c1], in_=yq[:, c0:c1])

        for h in range(2):
            add(0, h * HALF, HALF)
            store_y(slice(0, 1), h)
        nc.scalar.activation(pages[0][:].indirect(list_page[:]), rest[:, 2, :], COPY)
        for h in range(2):
            add(1, h * HALF, HALF)
            store_y(slice(1, 2), h)
            for t in (2, 3):
                for n in (2 * h, 2 * h + 1):
                    add(t, n * CHUNK, CHUNK)
            store_y(slice(2, 4), h)
        cast(nc.scalar.copy, 0, 0, CHUNK)
        cast(nc.scalar.copy, 1, 0, CHUNK)
        cast(nc.scalar.copy, 2, 0, SCALAR_SHARE)
        quantise(0, 0, CHUNK)
        cast(nc.vector.tensor_copy, 3, 0, CHUNK)
        cast(nc.vector.tensor_copy, 2, SCALAR_SHARE, CHUNK)
        quantise(1, 0, CHUNK)
        store_words(0, HALF)
        quantise(3, 0, CHUNK)
        store_words(3 * CHUNK, 4 * CHUNK)
        quantise(2, 0, CHUNK)
        store_words(2 * CHUNK, 3 * CHUNK)
        for q in range(4):
            queue = nc.sync if q < 2 else nc.scalar
            queue.dma_start(
                out=out_2[0, 4 * q : 4 * q + 4, :].bitcast(I32),
                in_=ysc[32 * q : 32 * q + 4, :].bitcast(I32),
            )
